import numpy as np
import ml_dtypes


def mxq(x, axis, fmt="e4m3"):
    dtype, down = {"e4m3": (ml_dtypes.float8_e4m3fn, 7), "e5m2": (ml_dtypes.float8_e5m2, 14)}[fmt]
    v = np.moveaxis(np.asarray(x, np.float32).astype(ml_dtypes.bfloat16).astype(np.float64), axis, -1)
    blocks = v.reshape(v.shape[:-1] + (-1, 32))
    amax = np.abs(blocks).max(-1, keepdims=True)
    byte = np.maximum(np.where(amax > 0, np.frexp(amax)[1] - 1 + 127, 0) - down, 1)
    scale = np.exp2(byte - 127.0)
    codes = (blocks / scale).astype(np.float32).astype(dtype).astype(np.float64)
    return np.moveaxis((codes * scale).reshape(v.shape), -1, axis)


WIDE = False


def mx_kscale(k):
    if not WIDE:
        return np.ones(k)
    levels = np.array([10, -10, 5, -5, 0])
    if k % 512:
        return np.exp2(np.random.permutation(np.resize(levels, k // 32))).repeat(32)
    a = np.empty((k // 512, 16))
    for p in range(k // 512):
        a[p, :8] = np.random.permutation(np.resize(levels, 8))
        for g in range(8):
            far = levels[np.abs(levels - a[p, g]) >= 10]
            a[p, g + 8] = far[np.random.randint(len(far))]
    return np.exp2(a.ravel()).repeat(32)


def f64(x):
    return np.asarray(x).astype(np.float64)


def striped8(idx):
    return np.concatenate([x.reshape(-1, 16).T for x in idx]).astype(np.uint16)


def runs(offs, k):
    lists = np.stack([offs[16 * r : 16 * r + 16].T.reshape(-1) for r in range(8)]).astype(np.int64)
    return lists[np.arange(k) % 512 // 64]


def pack_weight(w):
    k, n = w.shape
    w = f64(np.asarray(w, np.float32).astype(ml_dtypes.bfloat16)).reshape(k // 32, 32, n)
    amax = np.abs(w).max(1)
    byte = np.clip(np.where(amax > 0, np.frexp(amax)[1] - 1 + 127 - 7, 1), 1, 254)
    scaled = (w * np.exp2(127.0 - byte)[:, None, :]).reshape(k, n).astype(np.float32)
    words = np.ascontiguousarray(scaled.reshape(k // 512, 128, 4, n).transpose(0, 1, 3, 2)).astype(ml_dtypes.float8_e4m3fn).view(np.uint8)
    return words, np.ascontiguousarray(byte.astype(np.uint8).reshape(k // 512, 16, n))


def unpack_weight(words, scales):
    g, p, n, _ = words.shape
    vals = np.ascontiguousarray(words).view(ml_dtypes.float8_e4m3fn).astype(np.float64) * np.repeat(np.exp2(scales.astype(np.float64) - 127.0), 8, axis=1)[..., None]
    return vals.transpose(0, 1, 3, 2).reshape(g * 512, n)

def planes(y):
    n, m = y.shape
    v = y.astype(np.float32).astype(ml_dtypes.bfloat16).astype(np.float64).reshape(n // 32, 32, m)
    top = np.abs(v).max(1)
    byte = np.clip(np.where(top > 0, np.frexp(top)[1] - 1 + 127 - 7, 1), 1, 254)
    codes = (v * np.exp2(127.0 - byte)[:, None, :]).reshape(n, m).astype(np.float32).astype(ml_dtypes.float8_e4m3fn).view(np.uint8)
    words = codes.reshape(n // 512, 128, 4, m).transpose(0, 1, 3, 2)
    return np.ascontiguousarray(words), np.ascontiguousarray(byte.astype(np.uint8).reshape(n // 512, 16, m))


K, T, S, N, H, U = 512, 2048, 512, 512, 512, 512


def setup_inputs():
    n = np.random.standard_normal
    s = mx_kscale(K)[:, None]
    u = mx_kscale(H)
    packed_xT = pack_weight(n((K, T)) * s)
    packed_w1 = pack_weight(n((K, H)) / np.sqrt(K) / s)
    packed_w2 = pack_weight(n((H, N)) / np.sqrt(H) / u[:, None])
    return {
        "x_words": packed_xT[0],
        "x_scales": packed_xT[1],
        "w1_words": packed_w1[0],
        "w1_scales": packed_w1[1],
        "tab": n((H, U)).astype(np.float32),
        "gn": (np.random.uniform(0.5, 1.5, (H, 1)) * u[:, None]).astype(np.float32),
        "w2_words": packed_w2[0],
        "w2_scales": packed_w2[1],
        "offs": striped8(np.random.randint(0, T, (8, S))),
        "kind": striped8(np.random.randint(0, U, (8, S))),
        "n1": striped8(np.stack([np.random.permutation(S) for _ in range(8)])),
        "n2": striped8(np.stack([np.random.permutation(S) for _ in range(8)])),
    }


def reference(x_words, x_scales, w1_words, w1_scales, tab, gn, w2_words, w2_scales, offs, kind, n1, n2):
    xq = unpack_weight(x_words, x_scales)[np.arange(K)[:, None], runs(offs, K)]
    y = unpack_weight(w1_words, w1_scales).T @ xq
    bx = y + f64(tab)[np.arange(H)[:, None], runs(kind, H)]
    z = f64(gn) * (np.maximum(bx, np.minimum(bx[np.arange(H)[:, None], runs(n1, H)], bx[np.arange(H)[:, None], runs(n2, H)])))
    out_0 = unpack_weight(w2_words, w2_scales).T @ mxq(z, 0, "e4m3")
    return (out_0,) + planes(out_0)

@@ -1,0 +1,344 @@
+from contextlib import ExitStack
+
+import concourse.mybir as mybir
+from concourse.masks import make_identity
+
+F32 = mybir.dt.float32
+BF16 = mybir.dt.bfloat16
+I32 = mybir.dt.int32
+U32 = mybir.dt.uint32
+U16 = mybir.dt.uint16
+U8 = mybir.dt.uint8
+FP8X4 = mybir.dt.float8_e4m3fn_x4
+ALU = mybir.AluOpType
+COPY = mybir.ActivationFunctionType.Copy
+
+P = 128
+PACK = 4
+T = 2048
+S = 512
+H = 512
+UNIT = 128
+UNITS = S // UNIT
+HALF = 256
+FLOPS = 2 * 2 * 512 * 512 * 512
+
+
+def entries(lst, start, count):
+    return lst[:, start // 16 : (start + count) // 16]
+
+
+def tile_picked_hashkind_none_po_kernel(
+    tc, x_words, x_scales, w1_words, w1_scales, tab, gn, w2_words, w2_scales, offs, kind, n1, n2, out_0, out_1, out_2
+):
+    nc = tc.nc
+    with ExitStack() as ctx:
+        keep = ctx.enter_context(tc.tile_pool(name="keep", bufs=1))
+        ring = ctx.enter_context(tc.tile_pool(name="ring", bufs=2))
+        psum = ctx.enter_context(tc.psum_pool(name="psum", bufs=1))
+
+        offs_t = keep.tile([P, S // 16], U16, name="offs_t")
+        kind_t = keep.tile([P, S // 16], U16, name="kind_t")
+        n1_t = keep.tile([P, S // 16], U16, name="n1_t")
+        n2_t = keep.tile([P, S // 16], U16, name="n2_t")
+
+        xs_table = keep.tile([P, T], U8, name="xs_table", align_bytes=64)
+        xw_table = keep.tile([P, T], U32, name="xw_table", align_bytes=64)
+        xs_picked = keep.tile([P, S], U8, name="xs_picked", align_bytes=64)
+        xw_picked = keep.tile([P, S], U32, name="xw_picked", align_bytes=64)
+        x_plane = keep.tile([P, S], U8, name="x_plane", align_bytes=64)
+        w1_plane = keep.tile([P, H], U8, name="w1_plane", align_bytes=64)
+        w2_plane_raw = keep.tile([P, H], U8, name="w2_plane_raw", align_bytes=64)
+        w1_codes = keep.tile([P, H], U32, name="w1_codes", align_bytes=64)
+        w2_raw = keep.tile([P, H], U32, name="w2_raw", align_bytes=64)
+        w2_codes = keep.tile([P, H], U32, name="w2_codes", align_bytes=64)
+        w2_plane = keep.tile([P, H], U8, name="w2_plane", align_bytes=64)
+        tabs = [keep.tile([P, H], F32, name="tab%d" % t) for t in range(PACK)]
+        gain = keep.tile([P, PACK], F32, name="gain")
+        gain_step = keep.tile([P, PACK], F32, name="gain_step")
+        gain_sign = keep.tile([P, PACK], F32, name="gain_sign")
+        gain_size = keep.tile([P, PACK], F32, name="gain_size")
+        ident = keep.tile([P, P], F32, name="ident")
+
+        nc.vector.memset(xs_table[:].bitcast(I32), 0)
+        nc.gpsimd.memset(w1_plane[:].bitcast(I32), 0)
+        make_identity(nc, ident[:])
+        nc.vector.memset(x_plane[:].bitcast(I32), 0)
+        nc.vector.memset(w2_plane_raw[:].bitcast(I32), 0)
+
+        tab_rows = tab.rearrange("(p t) u -> t p u", t=PACK)
+
+        def load_words(queue, tile, words):
+            queue.dma_start(tile[:].bitcast(I32), words[0].rearrange("p n t -> p (n t)").bitcast(I32))
+
+        def load_plane(queues, tile, scales):
+            for q, queue in enumerate(queues):
+                queue.dma_start(
+                    tile[32 * q : 32 * q + 4, :].bitcast(I32),
+                    scales[0][4 * q : 4 * q + 4, :].bitcast(I32),
+                )
+
+        nc.sync.dma_start(offs_t[:], offs)
+        nc.sync.dma_start(xs_table[0:P:8, :].bitcast(I32), x_scales[0].bitcast(I32))
+        nc.sync.dma_start(kind_t[:], kind)
+        nc.sync.dma_start(tabs[0][:], tab_rows[0])
+        load_words(nc.sync, xw_table, x_words)
+        load_plane([nc.scalar, nc.scalar, nc.scalar, nc.sync], w1_plane, w1_scales)
+
+        nc.vector.tensor_copy(xs_picked[:], xs_table[:].indirect(offs_t[:]))
+        for r in range(4):
+            nc.scalar.dma_start(x_plane[r:P:32, :].bitcast(I32), xs_picked[8 * r : P : 32, :].bitcast(I32))
+
+        load_words(nc.sync, w1_codes, w1_words)
+        nc.sync.dma_start(tabs[1][:], tab_rows[1])
+        for t in range(2, PACK):
+            nc.sync.dma_start(tabs[t][:], tab_rows[t])
+        nc.sync.dma_start(gain[:], gn.rearrange("(p t) o -> p (t o)", t=PACK))
+        nc.sync.dma_start(n1_t[:], n1)
+        nc.sync.dma_start(n2_t[:], n2)
+        load_words(nc.sync, w2_raw, w2_words)
+        load_plane([nc.sync] * 4, w2_plane_raw, w2_scales)
+
+        nc.gpsimd.tensor_scalar(gain_step[:], gain[:], 0.0, 2.0, ALU.is_ge, ALU.mult)
+        nc.gpsimd.tensor_scalar(gain_sign[:], gain_step[:], 1.0, -1.0, ALU.mult, ALU.add)
+        nc.gpsimd.tensor_tensor(gain_size[:], gain[:], gain_sign[:], ALU.mult)
+
+        shifts = [keep.tile([P, S], F32, name="shift%d" % t) for t in range(PACK)]
+        shifts_turned = [keep.tile([P, UNITS, P], F32, name="shift_turned%d" % t) for t in range(PACK)]
+
+        def pick_shift(t):
+            for start in range(0, S, HALF):
+                nc.vector.tensor_copy(
+                    shifts[t][:, start : start + HALF], tabs[t][:].indirect(entries(kind_t, start, HALF))
+                )
+
+        products = [psum.tile([P, H], F32, name="product%d" % u) for u in range(UNITS)]
+        turns = [psum.tile([P, H], F32, name="turn%d" % i) for i in range(2)]
+
+        def turn_shift(t):
+            bank = products[0] if t == 0 else turns[t % 2]
+            for u in range(UNITS):
+                cols = slice(u * UNIT, (u + 1) * UNIT)
+                nc.tensor.transpose(bank[:, cols], shifts[t][:, cols], ident[:])
+            nc.scalar.activation(shifts_turned[t][:].rearrange("j u p -> j (u p)"), bank[:], COPY)
+
+        pick_shift(0)
+        turn_shift(0)
+        for start in range(0, S, HALF):
+            nc.vector.tensor_copy(
+                xw_picked[:, start : start + HALF], xw_table[:].indirect(entries(offs_t, start, HALF))
+            )
+
+        y_turned = [keep.tile([P, PACK, P], F32, name="y_turned%d" % u) for u in range(UNITS)]
+        for u in range(UNITS):
+            cols = slice(u * UNIT, (u + 1) * UNIT)
+            bank = products[u]
+            nc.tensor.matmul_mx(
+                out=bank[:],
+                lhsT=xw_picked[:, cols].bitcast(FP8X4),
+                lhsT_scale=x_plane[:, cols],
+                rhs=w1_codes[:].bitcast(FP8X4),
+                rhs_scale=w1_plane[:],
+                start=True,
+                stop=True,
+            )
+            nc.scalar.copy(y_turned[u][:], bank[:].rearrange("j (p t) -> j t p", t=PACK))
+
+        scaled = [keep.tile([P, S], F32, name="scaled%d" % t) for t in range(PACK)]
+        scaled_bf = keep.tile([P, 2, PACK, UNIT], BF16, name="scaled_bf")
+
+        def make_scaled(t):
+            bank = psum.tile([P, UNITS, P], F32, name="sum_bank", tag="sum", bufs=2)
+            for u in range(UNITS):
+                nc.tensor.matmul(bank[:, u, :], shifts_turned[t][:, u, :], ident[:], start=True, stop=False, is_transpose=True)
+                nc.tensor.matmul(bank[:, u, :], y_turned[u][:, t, :], ident[:], start=False, stop=True, is_transpose=True)
+            nc.scalar.activation(
+                scaled[t][:], bank[:].rearrange("p u j -> p (u j)"), COPY, scale=gain_size[:, t : t + 1]
+            )
+
+        for t in range(1, PACK):
+            pick_shift(t)
+        for t in range(PACK):
+            if t + 1 < PACK:
+                turn_shift(t + 1)
+            make_scaled(t)
+        for t in range(PACK):
+            nc.scalar.copy(scaled_bf[:, :, t, :], scaled[t][:, UNIT : 3 * UNIT].rearrange("p (u j) -> p u j", u=2))
+
+        nc.vector.tensor_copy(
+            w2_codes[:].bitcast(I32).rearrange("p (t m) -> p t m", t=PACK),
+            w2_raw[:].bitcast(I32).rearrange("p (m t) -> p t m", t=PACK),
+        )
+        nc.vector.tensor_copy(
+            w2_plane[:].rearrange("p (t m) -> p t m", t=PACK),
+            w2_plane_raw[:].rearrange("p (m t) -> p t m", t=PACK),
+        )
+
+        out_codes = keep.tile([P, S], U32, name="out_codes", align_bytes=64)
+        out_plane = keep.tile([P, S], U8, name="out_plane", align_bytes=64)
+        out_rows = out_0.rearrange("(p t) j -> p t j", t=PACK)
+        out_words = out_1[0].rearrange("p n t -> p (n t)").bitcast(I32)
+
+        work = [keep.tile([P, 2, PACK * UNIT], BF16, name="work%d" % u, align_bytes=64) for u in range(UNITS)]
+        early = keep.tile([P, 2, PACK * UNIT], BF16, name="early", align_bytes=64)
+        pair1 = keep.tile([P, 2, PACK * UNIT], BF16, name="pair1", align_bytes=64)
+        late = keep.tile([P, 2, PACK * UNIT], BF16, name="late", align_bytes=64)
+        lesser = keep.tile([P, PACK * UNIT], BF16, name="lesser")
+        larger = [keep.tile([P, PACK * UNIT], BF16, name="larger%d" % u) for u in range(2)]
+        z_codes = [keep.tile([P, UNIT], U32, name="z_codes%d" % u, align_bytes=64) for u in range(UNITS)]
+        z_plane = [keep.tile([P, UNIT], U8, name="z_plane%d" % u, align_bytes=64) for u in range(UNITS)]
+        out_grouped = [keep.tile([P, PACK * UNIT], BF16, name="out_grouped%d" % u, align_bytes=64) for u in range(UNITS)]
+
+        def part(ap, i):
+            return ap[:, i * UNIT : (i + 1) * UNIT]
+
+        def woven(ap):
+            return ap.rearrange("p (j t) -> p j t", t=PACK)
+
+        pairs = {1: pair1, 2: work[0]}
+        rooms = {}
+        for t in range(PACK):
+            tile = early if t < 2 else pair1
+            a = 2 * (t % 2)
+            rooms[0, t] = [part(tile[:, 0, :], a), part(tile[:, 1, :], a), part(tile[:, 0, :], a + 1), part(tile[:, 1, :], a + 1)]
+        rooms[3, 0] = [part(work[1][:, 0, :], 0), part(work[1][:, 1, :], 0), part(late[:, 0, :], 0), part(late[:, 1, :], 0)]
+        rooms[3, 1] = [part(work[1][:, 1, :], 1), part(work[1][:, 1, :], 2), part(late[:, 0, :], 1), part(late[:, 1, :], 1)]
+        rooms[3, 2] = [part(out_grouped[1][:], 0), part(out_grouped[1][:], 1), part(late[:, 0, :], 2), part(late[:, 1, :], 2)]
+        rooms[3, 3] = [part(work[2][:, 1, :], 0), part(work[2][:, 1, :], 1), part(late[:, 0, :], 3), part(late[:, 1, :], 3)]
+
+        def fetch(u, t, which):
+            target = part(pairs[u][:, which, :], t) if u in pairs else rooms[u, t][which]
+            lst = (n1_t, n2_t)[which]
+            nc.vector.tensor_copy(target, scaled[t][:].indirect(entries(lst, u * UNIT, UNIT)))
+
+        def weave_z(u):
+            nc.scalar.copy(woven(work[u][:, 1, :]), work[u][:, 0, :].rearrange("p (t j) -> p j t", t=PACK))
+
+        def min_row(u, t):
+            room = rooms[u, t]
+            nc.vector.tensor_tensor(room[2], room[0], room[1], ALU.min)
+
+        def max_row(u, t):
+            room = rooms[u, t]
+            nc.vector.tensor_tensor(room[3], room[2], part(scaled[t][:], u), ALU.max)
+            sign = gain_sign[:, t : t + 1]
+            if u == UNITS - 1:
+                nc.vector.tensor_scalar(woven(work[u][:, 1, :])[:, :, t], room[3], sign, None, ALU.mult)
+            else:
+                nc.scalar.activation(part(work[u][:, 0, :], t), room[3], COPY, scale=sign)
+                if t == PACK - 1:
+                    weave_z(u)
+
+        def min_unit(u):
+            nc.vector.tensor_tensor(lesser[:], pairs[u][:, 0, :], pairs[u][:, 1, :], ALU.min)
+
+        def max_unit(u):
+            nc.vector.tensor_tensor(
+                larger[u - 1][:], lesser[:], scaled_bf[:, u - 1, :, :].rearrange("p t j -> p (t j)"), ALU.max
+            )
+            for t in range(PACK):
+                nc.scalar.activation(
+                    part(work[u][:, 0, :], t), part(larger[u - 1][:], t), COPY, scale=gain_sign[:, t : t + 1]
+                )
+            weave_z(u)
+
+        def quantize_z(u):
+            nc.vector.quantize_mx(
+                out=z_codes[u][:].bitcast(FP8X4),
+                scales=z_plane[u][:],
+                in_=work[u][:, 1, :],
+            )
+
+        def second_product(u):
+            cols = slice(u * UNIT, (u + 1) * UNIT)
+            bank = products[u]
+            for t in range(PACK):
+                rows = slice(t * P, (t + 1) * P)
+                nc.tensor.matmul_mx(
+                    out=bank[:, rows],
+                    lhsT=w2_codes[:, rows].bitcast(FP8X4),
+                    lhsT_scale=w2_plane[:, rows],
+                    rhs=z_codes[u][:].bitcast(FP8X4),
+                    rhs_scale=z_plane[u][:],
+                    start=True,
+                    stop=True,
+                )
+            stepped = bank[:].rearrange("p (t j) -> p j t", t=PACK)
+            if u == UNITS - 1:
+                nc.vector.tensor_copy(woven(out_grouped[u][:]), stepped)
+            else:
+                nc.scalar.copy(woven(out_grouped[u][:]), stepped)
+            result = ring.tile([P, PACK, UNIT], F32, name="result")
+            nc.scalar.copy(result[:], bank[:].rearrange("p (t j) -> p t j", t=PACK))
+            nc.sync.dma_start(out_rows[:, :, cols], result[:])
+
+        def quantize_out(u):
+            cols = slice(u * UNIT, (u + 1) * UNIT)
+            nc.vector.quantize_mx(
+                out=out_codes[:, cols].bitcast(FP8X4),
+                scales=out_plane[:, cols],
+                in_=out_grouped[u][:],
+            )
+            nc.sync.dma_start(out_words[:, cols], out_codes[:, cols].bitcast(I32))
+
+        def product_of(u):
+            quantize_z(u)
+            second_product(u)
+
+        between = {
+            (0, 1, 0): [(min_row, 0, 0)], (0, 1, 1): [(max_row, 0, 0)],
+            (0, 2, 0): [(min_row, 0, 1)], (0, 2, 1): [(max_row, 0, 1)],
+        }
+        for t in range(PACK):
+            for which in range(2):
+                if t == 3 and which == 0:
+                    min_row(0, 2)
+                    max_row(0, 2)
+                fetch(0, t, which)
+                for call, x, y in between.get((0, t, which), []):
+                    call(x, y)
+        fetch(1, 0, 0)
+        min_row(0, 3)
+        fetch(1, 0, 1)
+        max_row(0, 3)
+        for t in range(1, PACK):
+            fetch(1, t, 0)
+            fetch(1, t, 1)
+        fetch(2, 0, 0)
+        min_unit(1)
+        product_of(0)
+        max_unit(1)
+        fetch(2, 0, 1)
+        for t in range(1, PACK):
+            fetch(2, t, 0)
+            fetch(2, t, 1)
+            if t == 2:
+                quantize_out(0)
+        fetch(3, 0, 0)
+        min_unit(2)
+        product_of(1)
+        max_unit(2)
+        fetch(3, 0, 1)
+        fetch(3, 1, 0)
+        min_row(3, 0)
+        fetch(3, 1, 1)
+        max_row(3, 0)
+        quantize_out(1)
+        fetch(3, 2, 0)
+        min_row(3, 1)
+        fetch(3, 2, 1)
+        max_row(3, 1)
+        product_of(2)
+        fetch(3, 3, 0)
+        min_row(3, 2)
+        fetch(3, 3, 1)
+        max_row(3, 2)
+        min_row(3, 3)
+        max_row(3, 3)
+        quantize_out(2)
+        product_of(3)
+        quantize_out(3)
+
+        for r in range(4):
+            queue = nc.sync if r % 2 == 0 else nc.scalar
+            queue.dma_start(out_2[0][r:16:4, :].bitcast(I32), out_plane[r:P:32, :].bitcast(I32))

@@ -42,7 +42,7 @@ def tile_picked_hashkind_none_po_kernel(
         n1_t = keep.tile([P, S // 16], U16, name="n1_t")
         n2_t = keep.tile([P, S // 16], U16, name="n2_t")
 
-        xs_table = keep.tile([P, T], U8, name="xs_table", align_bytes=64)
+        xs_table = keep.tile([P, T], U8, name="xs_table", tag="scales_then_shift", align_bytes=64)
         xw_table = keep.tile([P, T], U32, name="xw_table", align_bytes=64)
         xs_picked = keep.tile([P, S], U8, name="xs_picked", align_bytes=64)
         xw_picked = keep.tile([P, S], U32, name="xw_picked", align_bytes=64)
@@ -53,7 +53,7 @@ def tile_picked_hashkind_none_po_kernel(
         w2_raw = keep.tile([P, H], U32, name="w2_raw", align_bytes=64)
         w2_codes = keep.tile([P, H], U32, name="w2_codes", align_bytes=64)
         w2_plane = keep.tile([P, H], U8, name="w2_plane", align_bytes=64)
-        tabs = [keep.tile([P, H], F32, name="tab%d" % t) for t in range(PACK)]
+        tabs = [keep.tile([P, 2 * H], F32, name="tab%d" % t) for t in range(PACK)]
         gain = keep.tile([P, PACK], F32, name="gain")
         gain_step = keep.tile([P, PACK], F32, name="gain_step")
         gain_sign = keep.tile([P, PACK], F32, name="gain_sign")
@@ -65,6 +65,8 @@ def tile_picked_hashkind_none_po_kernel(
         make_identity(nc, ident[:])
         nc.vector.memset(x_plane[:].bitcast(I32), 0)
         nc.vector.memset(w2_plane_raw[:].bitcast(I32), 0)
+        for t in range(PACK):
+            nc.vector.memset(tabs[t][:, H : 2 * H].bitcast(I32), 0)
 
         tab_rows = tab.rearrange("(p t) u -> t p u", t=PACK)
 
@@ -79,9 +81,9 @@ def tile_picked_hashkind_none_po_kernel(
                 )
 
         nc.sync.dma_start(offs_t[:], offs)
-        nc.sync.dma_start(xs_table[0:P:8, :].bitcast(I32), x_scales[0].bitcast(I32))
         nc.sync.dma_start(kind_t[:], kind)
-        nc.sync.dma_start(tabs[0][:], tab_rows[0])
+        nc.sync.dma_start(tabs[0][:, 0:H], tab_rows[0])
+        nc.sync.dma_start(xs_table[0:P:8, :].bitcast(I32), x_scales[0].bitcast(I32))
         load_words(nc.sync, xw_table, x_words)
         load_plane([nc.scalar, nc.scalar, nc.scalar, nc.sync], w1_plane, w1_scales)
 
@@ -90,10 +92,10 @@ def tile_picked_hashkind_none_po_kernel(
             nc.scalar.dma_start(x_plane[r:P:32, :].bitcast(I32), xs_picked[8 * r : P : 32, :].bitcast(I32))
 
         load_words(nc.sync, w1_codes, w1_words)
-        nc.sync.dma_start(tabs[1][:], tab_rows[1])
-        for t in range(2, PACK):
-            nc.sync.dma_start(tabs[t][:], tab_rows[t])
+        nc.sync.dma_start(tabs[1][:, 0:H], tab_rows[1])
         nc.sync.dma_start(gain[:], gn.rearrange("(p t) o -> p (t o)", t=PACK))
+        for t in range(2, PACK):
+            nc.sync.dma_start(tabs[t][:, 0:H], tab_rows[t])
         nc.sync.dma_start(n1_t[:], n1)
         nc.sync.dma_start(n2_t[:], n2)
         load_words(nc.sync, w2_raw, w2_words)
@@ -103,33 +105,41 @@ def tile_picked_hashkind_none_po_kernel(
         nc.gpsimd.tensor_scalar(gain_sign[:], gain_step[:], 1.0, -1.0, ALU.mult, ALU.add)
         nc.gpsimd.tensor_tensor(gain_size[:], gain[:], gain_sign[:], ALU.mult)
 
-        shifts = [keep.tile([P, S], F32, name="shift%d" % t) for t in range(PACK)]
+        shifts = [keep.tile([P, S], F32, name="shift0", tag="scales_then_shift", align_bytes=64)]
+        shifts.extend(keep.tile([P, S], F32, name="shift%d" % t) for t in range(1, PACK))
         shifts_turned = [keep.tile([P, UNITS, P], F32, name="shift_turned%d" % t) for t in range(PACK)]
 
         def pick_shift(t):
-            for start in range(0, S, HALF):
-                nc.vector.tensor_copy(
-                    shifts[t][:, start : start + HALF], tabs[t][:].indirect(entries(kind_t, start, HALF))
-                )
+            nc.vector.tensor_copy(shifts[t][:], tabs[t][:].indirect(kind_t[:]))
 
         products = [psum.tile([P, H], F32, name="product%d" % u) for u in range(UNITS)]
-        turns = [psum.tile([P, H], F32, name="turn%d" % i) for i in range(2)]
+        sums = [psum.tile([P, S], F32, name="sum%d" % t) for t in range(PACK)]
+
+        turn_banks = {1: products[0], 2: products[3], 3: products[0]}
 
         def turn_shift(t):
-            bank = products[0] if t == 0 else turns[t % 2]
             for u in range(UNITS):
                 cols = slice(u * UNIT, (u + 1) * UNIT)
-                nc.tensor.transpose(bank[:, cols], shifts[t][:, cols], ident[:])
-            nc.scalar.activation(shifts_turned[t][:].rearrange("j u p -> j (u p)"), bank[:], COPY)
+                target = products[u][:, 0:P] if t == 0 else turn_banks[t][:, cols]
+                nc.tensor.transpose(target, shifts[t][:, cols], ident[:])
+                if t == 0:
+                    nc.scalar.activation(shifts_turned[t][:, u, :], target, COPY)
+            if t > 0:
+                nc.scalar.activation(shifts_turned[t][:].rearrange("j u p -> j (u p)"), turn_banks[t][:], COPY)
+
+        def turn_back(t):
+            for u in range(UNITS):
+                cols = slice(u * UNIT, (u + 1) * UNIT)
+                nc.tensor.matmul(
+                    sums[t][:, cols], shifts_turned[t][:, u, :], ident[:], start=u == 0, stop=False, is_transpose=True
+                )
 
         pick_shift(0)
         turn_shift(0)
-        for start in range(0, S, HALF):
-            nc.vector.tensor_copy(
-                xw_picked[:, start : start + HALF], xw_table[:].indirect(entries(offs_t, start, HALF))
-            )
+        turn_back(0)
+        nc.vector.tensor_copy(xw_picked[:], xw_table[:].indirect(offs_t[:]))
 
-        y_turned = [keep.tile([P, PACK, P], F32, name="y_turned%d" % u) for u in range(UNITS)]
+        y_turned = [keep.tile([P, PACK, P], F32, name="y_turned%d" % u, tag="y_turned%d" % u) for u in range(UNITS)]
         for u in range(UNITS):
             cols = slice(u * UNIT, (u + 1) * UNIT)
             bank = products[u]
@@ -145,25 +155,25 @@ def tile_picked_hashkind_none_po_kernel(
             nc.scalar.copy(y_turned[u][:], bank[:].rearrange("j (p t) -> j t p", t=PACK))
 
         scaled = [keep.tile([P, S], F32, name="scaled%d" % t) for t in range(PACK)]
-        scaled_bf = keep.tile([P, 2, PACK, UNIT], BF16, name="scaled_bf")
+        scaled_bf = keep.tile([P, PACK, 3 * UNIT], BF16, name="scaled_bf")
 
         def make_scaled(t):
-            bank = psum.tile([P, UNITS, P], F32, name="sum_bank", tag="sum", bufs=2)
             for u in range(UNITS):
-                nc.tensor.matmul(bank[:, u, :], shifts_turned[t][:, u, :], ident[:], start=True, stop=False, is_transpose=True)
-                nc.tensor.matmul(bank[:, u, :], y_turned[u][:, t, :], ident[:], start=False, stop=True, is_transpose=True)
-            nc.scalar.activation(
-                scaled[t][:], bank[:].rearrange("p u j -> p (u j)"), COPY, scale=gain_size[:, t : t + 1]
-            )
+                cols = slice(u * UNIT, (u + 1) * UNIT)
+                nc.tensor.matmul(
+                    sums[t][:, cols], y_turned[u][:, t, :], ident[:], start=False, stop=u == UNITS - 1, is_transpose=True
+                )
+            nc.scalar.activation(scaled[t][:], sums[t][:], COPY, scale=gain_size[:, t : t + 1])
+            nc.scalar.copy(scaled_bf[:, t, :], scaled[t][:, 0 : 3 * UNIT])
 
         for t in range(1, PACK):
             pick_shift(t)
         for t in range(PACK):
             if t + 1 < PACK:
                 turn_shift(t + 1)
+            if t > 0:
+                turn_back(t)
             make_scaled(t)
-        for t in range(PACK):
-            nc.scalar.copy(scaled_bf[:, :, t, :], scaled[t][:, UNIT : 3 * UNIT].rearrange("p (u j) -> p u j", u=2))
 
         nc.vector.tensor_copy(
             w2_codes[:].bitcast(I32).rearrange("p (t m) -> p t m", t=PACK),
@@ -179,15 +189,16 @@ def tile_picked_hashkind_none_po_kernel(
         out_rows = out_0.rearrange("(p t) j -> p t j", t=PACK)
         out_words = out_1[0].rearrange("p n t -> p (n t)").bitcast(I32)
 
-        work = [keep.tile([P, 2, PACK * UNIT], BF16, name="work%d" % u, align_bytes=64) for u in range(UNITS)]
-        early = keep.tile([P, 2, PACK * UNIT], BF16, name="early", align_bytes=64)
-        pair1 = keep.tile([P, 2, PACK * UNIT], BF16, name="pair1", align_bytes=64)
-        late = keep.tile([P, 2, PACK * UNIT], BF16, name="late", align_bytes=64)
-        lesser = keep.tile([P, PACK * UNIT], BF16, name="lesser")
-        larger = [keep.tile([P, PACK * UNIT], BF16, name="larger%d" % u) for u in range(2)]
+        signed = keep.tile([P, UNITS - 1, PACK, UNIT], BF16, name="signed", tag="y_turned3")
+        z_woven = [keep.tile([P, PACK * UNIT], BF16, name="z_woven%d" % u, align_bytes=64) for u in range(UNITS)]
+        out_woven = keep.tile([P, PACK * S], BF16, name="out_woven", align_bytes=64)
         z_codes = [keep.tile([P, UNIT], U32, name="z_codes%d" % u, align_bytes=64) for u in range(UNITS)]
         z_plane = [keep.tile([P, UNIT], U8, name="z_plane%d" % u, align_bytes=64) for u in range(UNITS)]
-        out_grouped = [keep.tile([P, PACK * UNIT], BF16, name="out_grouped%d" % u, align_bytes=64) for u in range(UNITS)]
+        wide = keep.tile([P, PACK, 4, HALF], BF16, name="wide")
+        pair = keep.tile([P, PACK, 2, UNIT], BF16, name="pair")
+        lesser = keep.tile([P, PACK, UNIT], BF16, name="lesser")
+        larger = keep.tile([P, PACK, UNIT], BF16, name="larger")
+        late = keep.tile([P, PACK, 2, UNIT], BF16, name="late")
 
         def part(ap, i):
             return ap[:, i * UNIT : (i + 1) * UNIT]
@@ -195,24 +206,21 @@ def tile_picked_hashkind_none_po_kernel(
         def woven(ap):
             return ap.rearrange("p (j t) -> p j t", t=PACK)
 
-        pairs = {1: pair1, 2: work[0]}
         rooms = {}
         for t in range(PACK):
-            tile = early if t < 2 else pair1
-            a = 2 * (t % 2)
-            rooms[0, t] = [part(tile[:, 0, :], a), part(tile[:, 1, :], a), part(tile[:, 0, :], a + 1), part(tile[:, 1, :], a + 1)]
-        rooms[3, 0] = [part(work[1][:, 0, :], 0), part(work[1][:, 1, :], 0), part(late[:, 0, :], 0), part(late[:, 1, :], 0)]
-        rooms[3, 1] = [part(work[1][:, 1, :], 1), part(work[1][:, 1, :], 2), part(late[:, 0, :], 1), part(late[:, 1, :], 1)]
-        rooms[3, 2] = [part(out_grouped[1][:], 0), part(out_grouped[1][:], 1), part(late[:, 0, :], 2), part(late[:, 1, :], 2)]
-        rooms[3, 3] = [part(work[2][:, 1, :], 0), part(work[2][:, 1, :], 1), part(late[:, 0, :], 3), part(late[:, 1, :], 3)]
+            rooms[0, t] = [wide[:, t, i, :] for i in range(4)]
+        holds = [rooms[0, 3][0], z_woven[0][:], z_woven[1][:], z_woven[2][:]]
+        for t in range(PACK):
+            rooms[3, t] = [part(holds[t], 0), part(holds[t], 1), late[:, t, 0, :], late[:, t, 1, :]]
+        spans = {0: HALF, 2: UNIT, 3: UNIT}
 
         def fetch(u, t, which):
-            target = part(pairs[u][:, which, :], t) if u in pairs else rooms[u, t][which]
+            target = pair[:, t, which, :] if u == 2 else rooms[u, t][which]
             lst = (n1_t, n2_t)[which]
-            nc.vector.tensor_copy(target, scaled[t][:].indirect(entries(lst, u * UNIT, UNIT)))
+            nc.vector.tensor_copy(target, scaled[t][:].indirect(entries(lst, u * UNIT, spans[u])))
 
         def weave_z(u):
-            nc.scalar.copy(woven(work[u][:, 1, :]), work[u][:, 0, :].rearrange("p (t j) -> p j t", t=PACK))
+            nc.scalar.copy(woven(z_woven[u][:]), signed[:, u, :, :].rearrange("p t j -> p j t"))
 
         def min_row(u, t):
             room = rooms[u, t]
@@ -220,42 +228,34 @@ def tile_picked_hashkind_none_po_kernel(
 
         def max_row(u, t):
             room = rooms[u, t]
-            nc.vector.tensor_tensor(room[3], room[2], part(scaled[t][:], u), ALU.max)
+            own = scaled_bf[:, t, 0:HALF] if u == 0 else part(scaled[t][:], u)
+            nc.vector.tensor_tensor(room[3], room[2], own, ALU.max)
+
+        def sign_row(u, t):
+            room = rooms[u, t]
             sign = gain_sign[:, t : t + 1]
             if u == UNITS - 1:
-                nc.vector.tensor_scalar(woven(work[u][:, 1, :])[:, :, t], room[3], sign, None, ALU.mult)
+                nc.vector.tensor_scalar(woven(z_woven[u][:])[:, :, t], room[3], sign, None, ALU.mult)
             else:
-                nc.scalar.activation(part(work[u][:, 0, :], t), room[3], COPY, scale=sign)
-                if t == PACK - 1:
-                    weave_z(u)
+                nc.scalar.activation(signed[:, 0:2, t, :], room[3].rearrange("p (u j) -> p u j", u=2), COPY, scale=sign)
 
-        def min_unit(u):
-            nc.vector.tensor_tensor(lesser[:], pairs[u][:, 0, :], pairs[u][:, 1, :], ALU.min)
+        def min_unit():
+            nc.vector.tensor_tensor(lesser[:], pair[:, :, 0, :], pair[:, :, 1, :], ALU.min)
 
-        def max_unit(u):
-            nc.vector.tensor_tensor(
-                larger[u - 1][:], lesser[:], scaled_bf[:, u - 1, :, :].rearrange("p t j -> p (t j)"), ALU.max
-            )
+        def max_unit():
+            nc.vector.tensor_tensor(larger[:], lesser[:], scaled_bf[:, :, HALF : 3 * UNIT], ALU.max)
+
+        def sign_unit():
             for t in range(PACK):
-                nc.scalar.activation(
-                    part(work[u][:, 0, :], t), part(larger[u - 1][:], t), COPY, scale=gain_sign[:, t : t + 1]
-                )
-            weave_z(u)
+                nc.scalar.activation(signed[:, 2, t, :], larger[:, t, :], COPY, scale=gain_sign[:, t : t + 1])
+            weave_z(2)
 
-        def quantize_z(u):
-            nc.vector.quantize_mx(
-                out=z_codes[u][:].bitcast(FP8X4),
-                scales=z_plane[u][:],
-                in_=work[u][:, 1, :],
-            )
-
-        def second_product(u):
-            cols = slice(u * UNIT, (u + 1) * UNIT)
-            bank = products[u]
+        def product_of(u, banks):
+            nc.vector.quantize_mx(out=z_codes[u][:].bitcast(FP8X4), scales=z_plane[u][:], in_=z_woven[u][:])
             for t in range(PACK):
                 rows = slice(t * P, (t + 1) * P)
                 nc.tensor.matmul_mx(
-                    out=bank[:, rows],
+                    out=banks[t][:, rows],
                     lhsT=w2_codes[:, rows].bitcast(FP8X4),
                     lhsT_scale=w2_plane[:, rows],
                     rhs=z_codes[u][:].bitcast(FP8X4),
@@ -263,81 +263,68 @@ def tile_picked_hashkind_none_po_kernel(
                     start=True,
                     stop=True,
                 )
-            stepped = bank[:].rearrange("p (t j) -> p j t", t=PACK)
-            if u == UNITS - 1:
-                nc.vector.tensor_copy(woven(out_grouped[u][:]), stepped)
-            else:
-                nc.scalar.copy(woven(out_grouped[u][:]), stepped)
-            result = ring.tile([P, PACK, UNIT], F32, name="result")
-            nc.scalar.copy(result[:], bank[:].rearrange("p (t j) -> p t j", t=PACK))
-            nc.sync.dma_start(out_rows[:, :, cols], result[:])
 
-        def quantize_out(u):
-            cols = slice(u * UNIT, (u + 1) * UNIT)
+        results = [keep.tile([P, PACK, UNIT], F32, name="result%d" % u) for u in range(UNITS)]
+
+        def weave_out(u):
+            nc.scalar.copy(woven(out_woven[:, u * S : (u + 1) * S]), products[u + 1][:].rearrange("p (t j) -> p j t", t=PACK))
+
+        def store_result(u):
+            nc.sync.dma_start(out_rows[:, :, u * UNIT : (u + 1) * UNIT], results[u][:])
+
+        def empty_out(u):
+            nc.scalar.copy(results[u][:], products[u + 1][:].rearrange("p (t j) -> p t j", t=PACK))
+            store_result(u)
+
+        def quantize_out(u, count):
+            cols = slice(u * UNIT, (u + count) * UNIT)
             nc.vector.quantize_mx(
                 out=out_codes[:, cols].bitcast(FP8X4),
                 scales=out_plane[:, cols],
-                in_=out_grouped[u][:],
+                in_=out_woven[:, u * S : (u + count) * S],
             )
             nc.sync.dma_start(out_words[:, cols], out_codes[:, cols].bitcast(I32))
 
-        def product_of(u):
-            quantize_z(u)
-            second_product(u)
-
-        between = {
-            (0, 1, 0): [(min_row, 0, 0)], (0, 1, 1): [(max_row, 0, 0)],
-            (0, 2, 0): [(min_row, 0, 1)], (0, 2, 1): [(max_row, 0, 1)],
-        }
         for t in range(PACK):
-            for which in range(2):
-                if t == 3 and which == 0:
-                    min_row(0, 2)
-                    max_row(0, 2)
-                fetch(0, t, which)
-                for call, x, y in between.get((0, t, which), []):
-                    call(x, y)
-        fetch(1, 0, 0)
-        min_row(0, 3)
-        fetch(1, 0, 1)
-        max_row(0, 3)
-        for t in range(1, PACK):
-            fetch(1, t, 0)
-            fetch(1, t, 1)
-        fetch(2, 0, 0)
-        min_unit(1)
-        product_of(0)
-        max_unit(1)
-        fetch(2, 0, 1)
-        for t in range(1, PACK):
+            fetch(0, t, 0)
+            fetch(0, t, 1)
             fetch(2, t, 0)
+            min_row(0, t)
             fetch(2, t, 1)
-            if t == 2:
-                quantize_out(0)
+            max_row(0, t)
+            sign_row(0, t)
+        weave_z(0)
+        weave_z(1)
+        min_unit()
         fetch(3, 0, 0)
-        min_unit(2)
-        product_of(1)
-        max_unit(2)
+        max_unit()
+        sign_unit()
         fetch(3, 0, 1)
-        fetch(3, 1, 0)
-        min_row(3, 0)
-        fetch(3, 1, 1)
-        max_row(3, 0)
-        quantize_out(1)
-        fetch(3, 2, 0)
-        min_row(3, 1)
-        fetch(3, 2, 1)
-        max_row(3, 1)
-        product_of(2)
-        fetch(3, 3, 0)
-        min_row(3, 2)
-        fetch(3, 3, 1)
-        max_row(3, 2)
+        for u in range(UNITS - 1):
+            product_of(u, [products[u + 1]] * PACK)
+            weave_out(u)
+            fetch(3, u + 1, 0)
+            min_row(3, u)
+            fetch(3, u + 1, 1)
+            max_row(3, u)
+            if u > 0:
+                sign_row(3, u - 1)
         min_row(3, 3)
+        sign_row(3, 2)
         max_row(3, 3)
-        quantize_out(2)
-        product_of(3)
-        quantize_out(3)
+        quantize_out(0, 2)
+        sign_row(3, 3)
+        for u in range(UNITS - 1):
+            empty_out(u)
+        last = UNITS - 1
+        product_of(last, [products[0], products[0], sums[0], sums[0]])
+        quantize_out(2, 1)
+        flat = results[last][:].rearrange("p t j -> p (t j)")
+        nc.vector.tensor_copy(flat[:, 0:HALF], products[0][:, 0:HALF])
+        nc.scalar.copy(flat[:, HALF:S], sums[0][:, HALF:S])
+        store_result(last)
+        nc.vector.tensor_copy(woven(out_woven[:, last * S : (last + 1) * S]), results[last][:].rearrange("p t j -> p j t"))
+        quantize_out(last, 1)
 
         for r in range(4):
             queue = nc.sync if r % 2 == 0 else nc.scalar

@@ -53,19 +53,23 @@ def tile_picked_hashkind_none_po_kernel(
         w2_raw = keep.tile([P, H], U32, name="w2_raw", align_bytes=64)
         w2_codes = keep.tile([P, H], U32, name="w2_codes", align_bytes=64)
         w2_plane = keep.tile([P, H], U8, name="w2_plane", align_bytes=64)
-        tabs = [keep.tile([P, 2 * H], F32, name="tab%d" % t) for t in range(PACK)]
+        tabs = [keep.tile([P, 2 * H if t in (1, 2) else H], F32, name="tab%d" % t) for t in range(PACK)]
         gain = keep.tile([P, PACK], F32, name="gain")
         gain_step = keep.tile([P, PACK], F32, name="gain_step")
         gain_sign = keep.tile([P, PACK], F32, name="gain_sign")
         gain_size = keep.tile([P, PACK], F32, name="gain_size")
         ident = keep.tile([P, P], F32, name="ident")
 
-        nc.vector.memset(xs_table[:].bitcast(I32), 0)
+        nc.vector.memset(xs_table[:, 0 : T // 2].bitcast(I32), 0)
+        nc.gpsimd.memset(xs_table[:, T // 2 : T].bitcast(I32), 0)
         nc.gpsimd.memset(w1_plane[:].bitcast(I32), 0)
+        warm = keep.tile([P, 2], F32, name="warm")
+        nc.gpsimd.memset(warm[:, 0:1], 0.0)
+        nc.scalar.activation(warm[:, 1:2], warm[:, 0:1], COPY)
         make_identity(nc, ident[:])
         nc.vector.memset(x_plane[:].bitcast(I32), 0)
         nc.vector.memset(w2_plane_raw[:].bitcast(I32), 0)
-        for t in range(PACK):
+        for t in (1, 2):
             nc.vector.memset(tabs[t][:, H : 2 * H].bitcast(I32), 0)
 
         tab_rows = tab.rearrange("(p t) u -> t p u", t=PACK)
@@ -82,8 +86,8 @@ def tile_picked_hashkind_none_po_kernel(
 
         nc.sync.dma_start(offs_t[:], offs)
         nc.sync.dma_start(kind_t[:], kind)
-        nc.sync.dma_start(tabs[0][:, 0:H], tab_rows[0])
         nc.sync.dma_start(xs_table[0:P:8, :].bitcast(I32), x_scales[0].bitcast(I32))
+        nc.sync.dma_start(tabs[0][:, 0:H], tab_rows[0])
         load_words(nc.sync, xw_table, x_words)
         load_plane([nc.scalar, nc.scalar, nc.scalar, nc.sync], w1_plane, w1_scales)
 
@@ -110,12 +114,16 @@ def tile_picked_hashkind_none_po_kernel(
         shifts_turned = [keep.tile([P, UNITS, P], F32, name="shift_turned%d" % t) for t in range(PACK)]
 
         def pick_shift(t):
-            nc.vector.tensor_copy(shifts[t][:], tabs[t][:].indirect(kind_t[:]))
+            count = S if t in (1, 2) else HALF
+            for start in range(0, S, count):
+                nc.vector.tensor_copy(
+                    shifts[t][:, start : start + count], tabs[t][:].indirect(entries(kind_t, start, count))
+                )
 
         products = [psum.tile([P, H], F32, name="product%d" % u) for u in range(UNITS)]
         sums = [psum.tile([P, S], F32, name="sum%d" % t) for t in range(PACK)]
 
-        turn_banks = {1: products[0], 2: products[3], 3: products[0]}
+        turn_banks = {1: products[3], 2: sums[0], 3: products[3]}
 
         def turn_shift(t):
             for u in range(UNITS):
@@ -136,8 +144,10 @@ def tile_picked_hashkind_none_po_kernel(
 
         pick_shift(0)
         turn_shift(0)
-        turn_back(0)
-        nc.vector.tensor_copy(xw_picked[:], xw_table[:].indirect(offs_t[:]))
+        for start in range(0, S, HALF):
+            nc.vector.tensor_copy(
+                xw_picked[:, start : start + HALF], xw_table[:].indirect(entries(offs_t, start, HALF))
+            )
 
         y_turned = [keep.tile([P, PACK, P], F32, name="y_turned%d" % u, tag="y_turned%d" % u) for u in range(UNITS)]
         for u in range(UNITS):
@@ -164,16 +174,20 @@ def tile_picked_hashkind_none_po_kernel(
                     sums[t][:, cols], y_turned[u][:, t, :], ident[:], start=False, stop=u == UNITS - 1, is_transpose=True
                 )
             nc.scalar.activation(scaled[t][:], sums[t][:], COPY, scale=gain_size[:, t : t + 1])
+
+        def round_scaled(t):
             nc.scalar.copy(scaled_bf[:, t, :], scaled[t][:, 0 : 3 * UNIT])
 
         for t in range(1, PACK):
             pick_shift(t)
         for t in range(PACK):
-            if t + 1 < PACK:
-                turn_shift(t + 1)
-            if t > 0:
-                turn_back(t)
+            turn_back(t)
             make_scaled(t)
+            if t == 0:
+                turn_shift(1)
+            round_scaled(t)
+            if t + 2 < PACK:
+                turn_shift(t + 2)
 
         nc.vector.tensor_copy(
             w2_codes[:].bitcast(I32).rearrange("p (t m) -> p t m", t=PACK),
@@ -185,12 +199,11 @@ def tile_picked_hashkind_none_po_kernel(
         )
 
         out_codes = keep.tile([P, S], U32, name="out_codes", align_bytes=64)
-        out_plane = keep.tile([P, S], U8, name="out_plane", align_bytes=64)
         out_rows = out_0.rearrange("(p t) j -> p t j", t=PACK)
         out_words = out_1[0].rearrange("p n t -> p (n t)").bitcast(I32)
 
         signed = keep.tile([P, UNITS - 1, PACK, UNIT], BF16, name="signed", tag="y_turned3")
-        z_woven = [keep.tile([P, PACK * UNIT], BF16, name="z_woven%d" % u, align_bytes=64) for u in range(UNITS)]
+        z_woven = [keep.tile([P, PACK * UNIT], BF16, name="z_woven%d" % u, tag="z_woven%d" % u, align_bytes=64) for u in range(UNITS)]
         out_woven = keep.tile([P, PACK * S], BF16, name="out_woven", align_bytes=64)
         z_codes = [keep.tile([P, UNIT], U32, name="z_codes%d" % u, align_bytes=64) for u in range(UNITS)]
         z_plane = [keep.tile([P, UNIT], U8, name="z_plane%d" % u, align_bytes=64) for u in range(UNITS)]
@@ -198,7 +211,7 @@ def tile_picked_hashkind_none_po_kernel(
         pair = keep.tile([P, PACK, 2, UNIT], BF16, name="pair")
         lesser = keep.tile([P, PACK, UNIT], BF16, name="lesser")
         larger = keep.tile([P, PACK, UNIT], BF16, name="larger")
-        late = keep.tile([P, PACK, 2, UNIT], BF16, name="late")
+        late = keep.tile([P, PACK + 1, UNIT], BF16, name="late")
 
         def part(ap, i):
             return ap[:, i * UNIT : (i + 1) * UNIT]
@@ -209,9 +222,11 @@ def tile_picked_hashkind_none_po_kernel(
         rooms = {}
         for t in range(PACK):
             rooms[0, t] = [wide[:, t, i, :] for i in range(4)]
-        holds = [rooms[0, 3][0], z_woven[0][:], z_woven[1][:], z_woven[2][:]]
-        for t in range(PACK):
-            rooms[3, t] = [part(holds[t], 0), part(holds[t], 1), late[:, t, 0, :], late[:, t, 1, :]]
+        first3, second3 = rooms[0, 3][0], rooms[0, 3][1]
+        rooms[3, 0] = [part(first3, 0), part(first3, 1), part(z_woven[0][:], 0), late[:, 0, :]]
+        rooms[3, 1] = [part(second3, 0), part(z_woven[0][:], 1), part(z_woven[1][:], 0), late[:, 1, :]]
+        rooms[3, 2] = [part(z_woven[1][:], 1), part(z_woven[1][:], 2), part(z_woven[2][:], 0), late[:, 2, :]]
+        rooms[3, 3] = [part(z_woven[2][:], 1), part(z_woven[2][:], 2), late[:, 4, :], late[:, 3, :]]
         spans = {0: HALF, 2: UNIT, 3: UNIT}
 
         def fetch(u, t, which):
@@ -300,24 +315,37 @@ def tile_picked_hashkind_none_po_kernel(
         max_unit()
         sign_unit()
         fetch(3, 0, 1)
-        for u in range(UNITS - 1):
-            product_of(u, [products[u + 1]] * PACK)
-            weave_out(u)
-            fetch(3, u + 1, 0)
-            min_row(3, u)
-            fetch(3, u + 1, 1)
-            max_row(3, u)
-            if u > 0:
-                sign_row(3, u - 1)
-        min_row(3, 3)
+        fetch(3, 1, 0)
+        product_of(0, [products[1]] * PACK)
+        empty_out(0)
+        min_row(3, 0)
+        fetch(3, 1, 1)
+        max_row(3, 0)
+        product_of(1, [products[2]] * PACK)
+        empty_out(1)
+        weave_out(0)
+        weave_out(1)
+        min_row(3, 1)
+        sign_row(3, 0)
+        max_row(3, 1)
+        fetch(3, 2, 0)
+        sign_row(3, 1)
+        fetch(3, 2, 1)
+        product_of(2, [products[3]] * PACK)
+        empty_out(2)
+        weave_out(2)
+        min_row(3, 2)
+        fetch(3, 3, 0)
+        max_row(3, 2)
+        fetch(3, 3, 1)
         sign_row(3, 2)
+        min_row(3, 3)
         max_row(3, 3)
-        quantize_out(0, 2)
         sign_row(3, 3)
-        for u in range(UNITS - 1):
-            empty_out(u)
         last = UNITS - 1
         product_of(last, [products[0], products[0], sums[0], sums[0]])
+        out_plane = keep.tile([P, S], U8, name="out_plane", tag="z_woven3", align_bytes=64)
+        quantize_out(0, 2)
         quantize_out(2, 1)
         flat = results[last][:].rearrange("p t j -> p (t j)")
         nc.vector.tensor_copy(flat[:, 0:HALF], products[0][:, 0:HALF])

from contextlib import ExitStack

import concourse.mybir as mybir
from concourse.masks import make_identity

F32 = mybir.dt.float32
BF16 = mybir.dt.bfloat16
I32 = mybir.dt.int32
U32 = mybir.dt.uint32
U16 = mybir.dt.uint16
U8 = mybir.dt.uint8
FP8X4 = mybir.dt.float8_e4m3fn_x4
ALU = mybir.AluOpType
COPY = mybir.ActivationFunctionType.Copy

P = 128
PACK = 4
T = 2048
S = 512
H = 512
UNIT = 128
UNITS = S // UNIT
HALF = 256
FLOPS = 2 * 2 * 512 * 512 * 512


def entries(lst, start, count):
    return lst[:, start // 16 : (start + count) // 16]


def tile_picked_hashkind_none_po_kernel(
    tc, x_words, x_scales, w1_words, w1_scales, tab, gn, w2_words, w2_scales, offs, kind, n1, n2, out_0, out_1, out_2
):
    nc = tc.nc
    with ExitStack() as ctx:
        keep = ctx.enter_context(tc.tile_pool(name="keep", bufs=1))
        ring = ctx.enter_context(tc.tile_pool(name="ring", bufs=2))
        psum = ctx.enter_context(tc.psum_pool(name="psum", bufs=1))

        offs_t = keep.tile([P, S // 16], U16, name="offs_t")
        kind_t = keep.tile([P, S // 16], U16, name="kind_t")
        n1_t = keep.tile([P, S // 16], U16, name="n1_t")
        n2_t = keep.tile([P, S // 16], U16, name="n2_t")

        xs_table = keep.tile([P, T], U8, name="xs_table", tag="scales_then_shift", align_bytes=64)
        xw_table = keep.tile([P, T], U32, name="xw_table", align_bytes=64)
        xs_picked = keep.tile([P, S], U8, name="xs_picked", align_bytes=64)
        xw_picked = keep.tile([P, S], U32, name="xw_picked", align_bytes=64)
        x_plane = keep.tile([P, S], U8, name="x_plane", align_bytes=64)
        w1_plane = keep.tile([P, H], U8, name="w1_plane", align_bytes=64)
        w2_plane_raw = keep.tile([P, H], U8, name="w2_plane_raw", align_bytes=64)
        w1_codes = keep.tile([P, H], U32, name="w1_codes", align_bytes=64)
        w2_raw = keep.tile([P, H], U32, name="w2_raw", align_bytes=64)
        w2_codes = keep.tile([P, H], U32, name="w2_codes", align_bytes=64)
        w2_plane = keep.tile([P, H], U8, name="w2_plane", align_bytes=64)
        tabs = [keep.tile([P, 2 * H if t in (1, 2) else H], F32, name="tab%d" % t) for t in range(PACK)]
        gain = keep.tile([P, PACK], F32, name="gain")
        gain_step = keep.tile([P, PACK], F32, name="gain_step")
        gain_sign = keep.tile([P, PACK], F32, name="gain_sign")
        gain_size = keep.tile([P, PACK], F32, name="gain_size")
        ident = keep.tile([P, P], F32, name="ident")

        nc.vector.memset(xs_table[:, 0 : T // 2].bitcast(I32), 0)
        nc.gpsimd.memset(xs_table[:, T // 2 : T].bitcast(I32), 0)
        nc.gpsimd.memset(w1_plane[:].bitcast(I32), 0)
        warm = keep.tile([P, 2], F32, name="warm")
        nc.gpsimd.memset(warm[:, 0:1], 0.0)
        nc.scalar.activation(warm[:, 1:2], warm[:, 0:1], COPY)
        make_identity(nc, ident[:])
        nc.vector.memset(x_plane[:].bitcast(I32), 0)
        nc.vector.memset(w2_plane_raw[:].bitcast(I32), 0)
        for t in (1, 2):
            nc.vector.memset(tabs[t][:, H : 2 * H].bitcast(I32), 0)

        tab_rows = tab.rearrange("(p t) u -> t p u", t=PACK)

        def load_words(queue, tile, words):
            queue.dma_start(tile[:].bitcast(I32), words[0].rearrange("p n t -> p (n t)").bitcast(I32))

        def load_plane(queues, tile, scales):
            for q, queue in enumerate(queues):
                queue.dma_start(
                    tile[32 * q : 32 * q + 4, :].bitcast(I32),
                    scales[0][4 * q : 4 * q + 4, :].bitcast(I32),
                )

        nc.sync.dma_start(offs_t[:], offs)
        nc.sync.dma_start(kind_t[:], kind)
        nc.sync.dma_start(xs_table[0:P:8, :].bitcast(I32), x_scales[0].bitcast(I32))
        nc.sync.dma_start(tabs[0][:, 0:H], tab_rows[0])
        load_words(nc.sync, xw_table, x_words)
        load_plane([nc.scalar, nc.scalar, nc.scalar, nc.sync], w1_plane, w1_scales)

        nc.vector.tensor_copy(xs_picked[:], xs_table[:].indirect(offs_t[:]))
        for r in range(4):
            nc.scalar.dma_start(x_plane[r:P:32, :].bitcast(I32), xs_picked[8 * r : P : 32, :].bitcast(I32))

        load_words(nc.sync, w1_codes, w1_words)
        nc.sync.dma_start(tabs[1][:, 0:H], tab_rows[1])
        nc.sync.dma_start(gain[:], gn.rearrange("(p t) o -> p (t o)", t=PACK))
        for t in range(2, PACK):
            nc.sync.dma_start(tabs[t][:, 0:H], tab_rows[t])
        nc.sync.dma_start(n1_t[:], n1)
        nc.sync.dma_start(n2_t[:], n2)
        load_words(nc.sync, w2_raw, w2_words)
        load_plane([nc.sync] * 4, w2_plane_raw, w2_scales)

        nc.gpsimd.tensor_scalar(gain_step[:], gain[:], 0.0, 2.0, ALU.is_ge, ALU.mult)
        nc.gpsimd.tensor_scalar(gain_sign[:], gain_step[:], 1.0, -1.0, ALU.mult, ALU.add)
        nc.gpsimd.tensor_tensor(gain_size[:], gain[:], gain_sign[:], ALU.mult)

        shifts = [keep.tile([P, S], F32, name="shift0", tag="scales_then_shift", align_bytes=64)]
        shifts.extend(keep.tile([P, S], F32, name="shift%d" % t) for t in range(1, PACK))
        shifts_turned = [keep.tile([P, UNITS, P], F32, name="shift_turned%d" % t) for t in range(PACK)]

        def pick_shift(t):
            count = S if t in (1, 2) else HALF
            for start in range(0, S, count):
                nc.vector.tensor_copy(
                    shifts[t][:, start : start + count], tabs[t][:].indirect(entries(kind_t, start, count))
                )

        products = [psum.tile([P, H], F32, name="product%d" % u) for u in range(UNITS)]
        sums = [psum.tile([P, S], F32, name="sum%d" % t) for t in range(PACK)]

        turn_banks = {1: products[3], 2: sums[0], 3: products[3]}

        def turn_shift(t):
            for u in range(UNITS):
                cols = slice(u * UNIT, (u + 1) * UNIT)
                target = products[u][:, 0:P] if t == 0 else turn_banks[t][:, cols]
                nc.tensor.transpose(target, shifts[t][:, cols], ident[:])
                if t == 0:
                    nc.scalar.activation(shifts_turned[t][:, u, :], target, COPY)
            if t > 0:
                nc.scalar.activation(shifts_turned[t][:].rearrange("j u p -> j (u p)"), turn_banks[t][:], COPY)

        def turn_back(t):
            for u in range(UNITS):
                cols = slice(u * UNIT, (u + 1) * UNIT)
                nc.tensor.matmul(
                    sums[t][:, cols], shifts_turned[t][:, u, :], ident[:], start=u == 0, stop=False, is_transpose=True
                )

        pick_shift(0)
        turn_shift(0)
        for start in range(0, S, HALF):
            nc.vector.tensor_copy(
                xw_picked[:, start : start + HALF], xw_table[:].indirect(entries(offs_t, start, HALF))
            )

        y_turned = [keep.tile([P, PACK, P], F32, name="y_turned%d" % u, tag="y_turned%d" % u) for u in range(UNITS)]
        for u in range(UNITS):
            cols = slice(u * UNIT, (u + 1) * UNIT)
            bank = products[u]
            nc.tensor.matmul_mx(
                out=bank[:],
                lhsT=xw_picked[:, cols].bitcast(FP8X4),
                lhsT_scale=x_plane[:, cols],
                rhs=w1_codes[:].bitcast(FP8X4),
                rhs_scale=w1_plane[:],
                start=True,
                stop=True,
            )
            nc.scalar.copy(y_turned[u][:], bank[:].rearrange("j (p t) -> j t p", t=PACK))

        scaled = [keep.tile([P, S], F32, name="scaled%d" % t) for t in range(PACK)]
        scaled_bf = keep.tile([P, PACK, 3 * UNIT], BF16, name="scaled_bf")

        def make_scaled(t):
            for u in range(UNITS):
                cols = slice(u * UNIT, (u + 1) * UNIT)
                nc.tensor.matmul(
                    sums[t][:, cols], y_turned[u][:, t, :], ident[:], start=False, stop=u == UNITS - 1, is_transpose=True
                )
            nc.scalar.activation(scaled[t][:], sums[t][:], COPY, scale=gain_size[:, t : t + 1])

        def round_scaled(t):
            nc.scalar.copy(scaled_bf[:, t, :], scaled[t][:, 0 : 3 * UNIT])

        for t in range(1, PACK):
            pick_shift(t)
        for t in range(PACK):
            turn_back(t)
            make_scaled(t)
            if t == 0:
                turn_shift(1)
            round_scaled(t)
            if t + 2 < PACK:
                turn_shift(t + 2)

        nc.vector.tensor_copy(
            w2_codes[:].bitcast(I32).rearrange("p (t m) -> p t m", t=PACK),
            w2_raw[:].bitcast(I32).rearrange("p (m t) -> p t m", t=PACK),
        )
        nc.vector.tensor_copy(
            w2_plane[:].rearrange("p (t m) -> p t m", t=PACK),
            w2_plane_raw[:].rearrange("p (m t) -> p t m", t=PACK),
        )

        out_codes = keep.tile([P, S], U32, name="out_codes", align_bytes=64)
        out_rows = out_0.rearrange("(p t) j -> p t j", t=PACK)
        out_words = out_1[0].rearrange("p n t -> p (n t)").bitcast(I32)

        signed = keep.tile([P, UNITS - 1, PACK, UNIT], BF16, name="signed", tag="y_turned3")
        z_woven = [keep.tile([P, PACK * UNIT], BF16, name="z_woven%d" % u, tag="z_woven%d" % u, align_bytes=64) for u in range(UNITS)]
        out_woven = keep.tile([P, PACK * S], BF16, name="out_woven", align_bytes=64)
        z_codes = [keep.tile([P, UNIT], U32, name="z_codes%d" % u, align_bytes=64) for u in range(UNITS)]
        z_plane = [keep.tile([P, UNIT], U8, name="z_plane%d" % u, align_bytes=64) for u in range(UNITS)]
        wide = keep.tile([P, PACK, 4, HALF], BF16, name="wide")
        pair = keep.tile([P, PACK, 2, UNIT], BF16, name="pair")
        lesser = keep.tile([P, PACK, UNIT], BF16, name="lesser")
        larger = keep.tile([P, PACK, UNIT], BF16, name="larger")
        late = keep.tile([P, PACK + 1, UNIT], BF16, name="late")

        def part(ap, i):
            return ap[:, i * UNIT : (i + 1) * UNIT]

        def woven(ap):
            return ap.rearrange("p (j t) -> p j t", t=PACK)

        rooms = {}
        for t in range(PACK):
            rooms[0, t] = [wide[:, t, i, :] for i in range(4)]
        first3, second3 = rooms[0, 3][0], rooms[0, 3][1]
        rooms[3, 0] = [part(first3, 0), part(first3, 1), part(z_woven[0][:], 0), late[:, 0, :]]
        rooms[3, 1] = [part(second3, 0), part(z_woven[0][:], 1), part(z_woven[1][:], 0), late[:, 1, :]]
        rooms[3, 2] = [part(z_woven[1][:], 1), part(z_woven[1][:], 2), part(z_woven[2][:], 0), late[:, 2, :]]
        rooms[3, 3] = [part(z_woven[2][:], 1), part(z_woven[2][:], 2), late[:, 4, :], late[:, 3, :]]
        spans = {0: HALF, 2: UNIT, 3: UNIT}

        def fetch(u, t, which):
            target = pair[:, t, which, :] if u == 2 else rooms[u, t][which]
            lst = (n1_t, n2_t)[which]
            nc.vector.tensor_copy(target, scaled[t][:].indirect(entries(lst, u * UNIT, spans[u])))

        def weave_z(u):
            nc.scalar.copy(woven(z_woven[u][:]), signed[:, u, :, :].rearrange("p t j -> p j t"))

        def min_row(u, t):
            room = rooms[u, t]
            nc.vector.tensor_tensor(room[2], room[0], room[1], ALU.min)

        def max_row(u, t):
            room = rooms[u, t]
            own = scaled_bf[:, t, 0:HALF] if u == 0 else part(scaled[t][:], u)
            nc.vector.tensor_tensor(room[3], room[2], own, ALU.max)

        def sign_row(u, t):
            room = rooms[u, t]
            sign = gain_sign[:, t : t + 1]
            if u == UNITS - 1:
                nc.vector.tensor_scalar(woven(z_woven[u][:])[:, :, t], room[3], sign, None, ALU.mult)
            else:
                nc.scalar.activation(signed[:, 0:2, t, :], room[3].rearrange("p (u j) -> p u j", u=2), COPY, scale=sign)

        def min_unit():
            nc.vector.tensor_tensor(lesser[:], pair[:, :, 0, :], pair[:, :, 1, :], ALU.min)

        def max_unit():
            nc.vector.tensor_tensor(larger[:], lesser[:], scaled_bf[:, :, HALF : 3 * UNIT], ALU.max)

        def sign_unit():
            for t in range(PACK):
                nc.scalar.activation(signed[:, 2, t, :], larger[:, t, :], COPY, scale=gain_sign[:, t : t + 1])
            weave_z(2)

        def product_of(u, banks):
            nc.vector.quantize_mx(out=z_codes[u][:].bitcast(FP8X4), scales=z_plane[u][:], in_=z_woven[u][:])
            for t in range(PACK):
                rows = slice(t * P, (t + 1) * P)
                nc.tensor.matmul_mx(
                    out=banks[t][:, rows],
                    lhsT=w2_codes[:, rows].bitcast(FP8X4),
                    lhsT_scale=w2_plane[:, rows],
                    rhs=z_codes[u][:].bitcast(FP8X4),
                    rhs_scale=z_plane[u][:],
                    start=True,
                    stop=True,
                )

        results = [keep.tile([P, PACK, UNIT], F32, name="result%d" % u) for u in range(UNITS)]

        def weave_out(u):
            nc.scalar.copy(woven(out_woven[:, u * S : (u + 1) * S]), products[u + 1][:].rearrange("p (t j) -> p j t", t=PACK))

        def store_result(u):
            nc.sync.dma_start(out_rows[:, :, u * UNIT : (u + 1) * UNIT], results[u][:])

        def empty_out(u):
            nc.scalar.copy(results[u][:], products[u + 1][:].rearrange("p (t j) -> p t j", t=PACK))
            store_result(u)

        def quantize_out(u, count):
            cols = slice(u * UNIT, (u + count) * UNIT)
            nc.vector.quantize_mx(
                out=out_codes[:, cols].bitcast(FP8X4),
                scales=out_plane[:, cols],
                in_=out_woven[:, u * S : (u + count) * S],
            )
            nc.sync.dma_start(out_words[:, cols], out_codes[:, cols].bitcast(I32))

        for t in range(PACK):
            fetch(0, t, 0)
            fetch(0, t, 1)
            fetch(2, t, 0)
            min_row(0, t)
            fetch(2, t, 1)
            max_row(0, t)
            sign_row(0, t)
        weave_z(0)
        weave_z(1)
        min_unit()
        fetch(3, 0, 0)
        max_unit()
        sign_unit()
        fetch(3, 0, 1)
        fetch(3, 1, 0)
        product_of(0, [products[1]] * PACK)
        empty_out(0)
        min_row(3, 0)
        fetch(3, 1, 1)
        max_row(3, 0)
        product_of(1, [products[2]] * PACK)
        empty_out(1)
        weave_out(0)
        weave_out(1)
        min_row(3, 1)
        sign_row(3, 0)
        max_row(3, 1)
        fetch(3, 2, 0)
        sign_row(3, 1)
        fetch(3, 2, 1)
        product_of(2, [products[3]] * PACK)
        empty_out(2)
        weave_out(2)
        min_row(3, 2)
        fetch(3, 3, 0)
        max_row(3, 2)
        fetch(3, 3, 1)
        sign_row(3, 2)
        min_row(3, 3)
        max_row(3, 3)
        sign_row(3, 3)
        last = UNITS - 1
        product_of(last, [products[0], products[0], sums[0], sums[0]])
        out_plane = keep.tile([P, S], U8, name="out_plane", tag="z_woven3", align_bytes=64)
        quantize_out(0, 2)
        quantize_out(2, 1)
        flat = results[last][:].rearrange("p t j -> p (t j)")
        nc.vector.tensor_copy(flat[:, 0:HALF], products[0][:, 0:HALF])
        nc.scalar.copy(flat[:, HALF:S], sums[0][:, HALF:S])
        store_result(last)
        nc.vector.tensor_copy(woven(out_woven[:, last * S : (last + 1) * S]), results[last][:].rearrange("p t j -> p j t"))
        quantize_out(last, 1)

        for r in range(4):
            queue = nc.sync if r % 2 == 0 else nc.scalar
            queue.dma_start(out_2[0][r:16:4, :].bitcast(I32), out_plane[r:P:32, :].bitcast(I32))
